import numpy as np
import ml_dtypes


def mxq(x, axis, fmt="e4m3"):
    dtype, down = {"e4m3": (ml_dtypes.float8_e4m3fn, 7), "e5m2": (ml_dtypes.float8_e5m2, 14)}[fmt]
    v = np.moveaxis(np.asarray(x, np.float32).astype(ml_dtypes.bfloat16).astype(np.float64), axis, -1)
    blocks = v.reshape(v.shape[:-1] + (-1, 32))
    amax = np.abs(blocks).max(-1, keepdims=True)
    byte = np.maximum(np.where(amax > 0, np.frexp(amax)[1] - 1 + 127, 0) - down, 1)
    scale = np.exp2(byte - 127.0)
    codes = (blocks / scale).astype(np.float32).astype(dtype).astype(np.float64)
    return np.moveaxis((codes * scale).reshape(v.shape), -1, axis)


WIDE = False


def mx_kscale(k):
    if not WIDE:
        return np.ones(k)
    levels = np.array([30, -30])
    if k % 512:
        return np.exp2(np.random.permutation(np.resize(levels, k // 32))).repeat(32)
    a = np.empty((k // 512, 16))
    for p in range(k // 512):
        a[p, :8] = np.random.permutation(np.resize(levels, 8))
        for g in range(8):
            far = levels[np.abs(levels - a[p, g]) >= 10]
            a[p, g + 8] = far[np.random.randint(len(far))]
    return np.exp2(a.ravel()).repeat(32)


def f64(x):
    return np.asarray(x).astype(np.float64)


def striped(idx):
    return np.tile(np.asarray(idx).reshape(-1, 16).T, (8, 1)).astype(np.uint16)


def unstriped(offs):
    return offs[:16].T.reshape(-1).astype(np.int64)


E2M1 = np.array([0.0, 0.5, 1.0, 1.5, 2.0, 3.0, 4.0, 6.0, -0.0, -0.5, -1.0, -1.5, -2.0, -3.0, -4.0, -6.0])


def pack_weight(w, fmt):
    k, n = w.shape
    w = f64(np.asarray(w, np.float32).astype(ml_dtypes.bfloat16)).reshape(k // 32, 32, n)
    amax = np.abs(w).max(1)
    if fmt == "e4m3":
        byte = np.frexp(amax)[1] - 1 + 127 - 7
    else:
        mant, ex = np.frexp(amax / 6.0)
        byte = np.where(mant > 0.5, ex, ex - 1) + 127
    byte = np.clip(np.where(amax > 0, byte, 1), 1, 254)
    scaled = (w * np.exp2(127.0 - byte)[:, None, :]).reshape(k, n).astype(np.float32)
    by_word = np.ascontiguousarray(scaled.reshape(k // 512, 128, 4, n).transpose(0, 1, 3, 2))
    if fmt == "e4m3":
        words = by_word.astype(ml_dtypes.float8_e4m3fn).view(np.uint8)
    else:
        c = by_word.astype(ml_dtypes.float4_e2m1fn).view(np.uint8) & 0xF
        words = (c[..., 0::2] | (c[..., 1::2] << 4)).reshape(k // 512, 128, 2 * n)
    return np.ascontiguousarray(words), np.ascontiguousarray(byte.astype(np.uint8).reshape(k // 512, 16, n))


def unpack_weight(words, scales, fmt):
    g, _, n = scales.shape
    words = np.ascontiguousarray(words).reshape(g, 128, n, -1)
    if fmt == "e4m3":
        vals = words.view(ml_dtypes.float8_e4m3fn).astype(np.float64)
    else:
        nib = np.empty((g, 128, n, 4), np.uint8)
        nib[..., 0::2] = words & 0xF
        nib[..., 1::2] = words >> 4
        vals = E2M1[nib]
    vals = vals * np.repeat(np.exp2(scales.astype(np.float64) - 127.0), 8, axis=1)[..., None]
    return vals.transpose(0, 1, 3, 2).reshape(g * 512, n)


N, K, T, J = 1024, 512, 1024, 512


def setup_inputs():
    n = np.random.standard_normal
    idx = np.random.permutation(T)[:J]
    fn = mx_kscale(N)
    wp = pack_weight(n((N, K)) * 1 / np.sqrt(N) * fn[:, None], "e2m1")
    return {
        "g": (n((N, T)) * np.exp(0.5 * n((1, T))) / fn[:, None]).astype(np.float32),
        "sv": (n((N, T))).astype(np.float32),
        "w_words": wp[0],
        "w_scales": wp[1],
        "run": (0.3 * n((K, T))).astype(np.float32),
        "offs": striped(idx),
    }


def reference(g, sv, w_words, w_scales, run, offs):
    idx = unstriped(offs)
    wu = unpack_weight(w_words, w_scales, "e2m1")
    d = 2.0 * f64(g)[:, idx] * np.maximum(f64(sv)[:, idx], 0.0)
    dq = mxq(d, 0, "e5m2")
    p = wu.T @ dq
    pp = np.zeros((K, T))
    pp[:, idx] = p
    y = pp + f64(run)
    return y

@@ -1,0 +1,140 @@
+from contextlib import ExitStack
+
+import concourse.mybir as mybir
+
+N, K, T, J = 1024, 512, 1024, 512
+FLOPS = 2 * N * K * J
+
+F32 = mybir.dt.float32
+BF16 = mybir.dt.bfloat16
+I32 = mybir.dt.int32
+U32 = mybir.dt.uint32
+U16 = mybir.dt.uint16
+U8 = mybir.dt.uint8
+E5M2 = mybir.dt.float8_e5m2_x4
+E2M1 = mybir.dt.float4_e2m1fn_x4
+ACT = mybir.ActivationFunctionType
+ALU = mybir.AluOpType
+
+P = 128
+PACK = 4
+PASSES = N // (P * PACK)
+PLANES = PASSES * PACK
+HALF = J // 2
+AHEAD = 2
+
+
+def tile_moe_expert_input_gradient_rectified_kernel(tc, g, sv, w_words, w_scales, run, offs, out):
+    nc = tc.nc
+    with ExitStack() as ctx:
+        keep = ctx.enter_context(tc.tile_pool(name="keep", bufs=1))
+        psum = ctx.enter_context(tc.psum_pool(name="psum", bufs=2))
+
+        offsets = keep.tile([P, J // 16], U16, name="offsets")
+        nc.sync.dma_start(offsets[:], offs)
+
+        g_rows = g.rearrange("(z p r) t -> z r p t", z=PASSES, r=PACK)
+        sv_rows = sv.rearrange("(z p r) t -> z r p t", z=PASSES, r=PACK)
+        g_sb = [keep.tile([P, T], F32, name="g%d" % i) for i in range(PLANES)]
+        sv_sb = [keep.tile([P, T], F32, name="sv%d" % i) for i in range(PLANES)]
+        words = keep.tile([P, PASSES, 2 * K], U8, name="words", align_bytes=64)
+        scales = keep.tile([P, PASSES, K], U8, name="scales", align_bytes=64)
+        run_sb = [keep.tile([P, T], F32, name="run%d" % m) for m in range(K // P)]
+        placed = [keep.tile([P, T], F32, name="placed%d" % m) for m in range(K // P)]
+
+        nc.vector.memset(scales[:].bitcast(I32), 0)
+        for m in range(K // P):
+            (nc.vector if m < 2 else nc.gpsimd).memset(placed[m][:], 0.0)
+
+        for i in range(PLANES + AHEAD):
+            if i < PLANES:
+                nc.sync.dma_start(sv_sb[i][:], sv_rows[i // PACK, i % PACK])
+            if i >= AHEAD:
+                nc.sync.dma_start(g_sb[i - AHEAD][:], g_rows[(i - AHEAD) // PACK, (i - AHEAD) % PACK])
+        nc.sync.dma_start(words[:].bitcast(I32), w_words.rearrange("z p b -> p z b").bitcast(I32))
+        scale_rows = w_scales.rearrange("z (q r) c -> r q z c", r=4).bitcast(I32)
+        for r in range(4):
+            nc.sync.dma_start(scales[r:P:32].bitcast(I32), scale_rows[r])
+        for m in range(K // P):
+            nc.sync.dma_start(run_sb[m][:], run[m * P:(m + 1) * P, :])
+
+        picked = [keep.tile([P, J], F32, name="picked%d" % i) for i in range(PLANES)]
+        rect = [keep.tile([P, J], F32, name="rect%d" % i) for i in range(PLANES)]
+        d32 = [keep.tile([P, PACK, J], F32, name="d32_%d" % z) for z in range(PASSES)]
+        d16 = [keep.tile([P, J, PACK], BF16, name="d16_%d" % z, align_bytes=64) for z in range(PASSES)]
+        codes = [keep.tile([P, J], U32, name="codes%d" % z, align_bytes=64) for z in range(PASSES)]
+        d_scales = [keep.tile([P, J], U8, name="d_scales%d" % z, align_bytes=64) for z in range(PASSES)]
+        prod = [keep.tile([P, J], F32, name="prod%d" % m) for m in range(K // P)]
+
+        def pick_sv(i):
+            nc.vector.tensor_copy(picked[i][:], sv_sb[i][:].indirect(offsets[:]))
+            nc.scalar.activation(rect[i][:], picked[i][:], ACT.Relu, scale=2.0)
+
+        def product(i, lo, hi):
+            nc.vector.tensor_tensor(d32[i // PACK][:, i % PACK, lo:hi], g_sb[i][:].indirect(offsets[:, lo // 16:hi // 16]),
+                                    rect[i][:, lo:hi], ALU.mult)
+
+        def weave_scalar(z, lo, hi):
+            nc.scalar.copy(d16[z][:, lo:hi, :], d32[z][:, :, lo:hi].rearrange("p r j -> p j r"))
+
+        def weave_vector(z, lo, hi):
+            nc.vector.tensor_copy(d16[z][:, lo:hi, :], d32[z][:, :, lo:hi].rearrange("p r j -> p j r"))
+
+        def quantize(z, lo, hi):
+            nc.vector.quantize_mx(out=codes[z][:, lo:hi].bitcast(E5M2), scales=d_scales[z][:, lo:hi],
+                                  in_=d16[z][:, lo:hi, :].rearrange("p j r -> p (j r)"))
+
+        def multiply(acc, m, z):
+            nc.tensor.matmul_mx(out=acc[:], lhsT=words[:, z, 2 * P * m:2 * P * (m + 1)].bitcast(E2M1),
+                                lhsT_scale=scales[:, z, P * m:P * (m + 1)],
+                                rhs=codes[z][:].bitcast(E5M2), rhs_scale=d_scales[z][:],
+                                start=(z == 0), stop=(z == PASSES - 1))
+
+        def scatter(m, lo, hi):
+            nc.vector.tensor_copy(placed[m][:].indirect(offsets[:, lo // 16:hi // 16]), prod[m][:, lo:hi])
+
+        def finish(engine, m, lo, hi):
+            engine.tensor_tensor(run_sb[m][:, lo:hi], placed[m][:, lo:hi], run_sb[m][:, lo:hi], ALU.add)
+            nc.sync.dma_start(out[m * P:(m + 1) * P, lo:hi], run_sb[m][:, lo:hi])
+
+        for i in range(PLANES + AHEAD):
+            if i < PLANES:
+                pick_sv(i)
+            k = i - AHEAD
+            if 0 <= k < PLANES - 1:
+                product(k, 0, J)
+            if k == PACK - 1:
+                weave_scalar(0, 0, HALF)
+            if k == PACK:
+                weave_scalar(0, HALF, J)
+            if k == PACK + 1:
+                quantize(0, 0, J)
+        product(PLANES - 1, 0, HALF)
+        weave_scalar(1, 0, HALF)
+        product(PLANES - 1, HALF, J)
+        weave_vector(1, HALF, J)
+        quantize(1, 0, HALF)
+        quantize(1, HALF, J)
+
+        acc = []
+        for m in range(K // P):
+            acc.append(psum.tile([P, J], F32, name="acc"))
+            for z in range(PASSES):
+                multiply(acc[m], m, z)
+            if m == 0:
+                nc.scalar.copy(prod[0][:, :HALF], acc[0][:, :HALF])
+            else:
+                nc.scalar.copy(prod[m][:], acc[m][:])
+            if m == 1:
+                nc.scalar.copy(prod[0][:, HALF:], acc[0][:, HALF:])
+
+        scatter(0, 0, HALF)
+        scatter(1, 0, J)
+        finish(nc.gpsimd, 1, 0, T)
+        scatter(0, HALF, J)
+        finish(nc.gpsimd, 0, 0, T)
+        scatter(2, 0, J)
+        finish(nc.gpsimd, 2, 0, T)
+        scatter(3, 0, J)
+        finish(nc.vector, 3, 0, T // 2)
+        finish(nc.vector, 3, T // 2, T)

@@ -21,14 +21,15 @@ PACK = 4
 PASSES = N // (P * PACK)
 PLANES = PASSES * PACK
 HALF = J // 2
-AHEAD = 2
+QUARTER = J // 4
+FUSED = 3
 
 
 def tile_moe_expert_input_gradient_rectified_kernel(tc, g, sv, w_words, w_scales, run, offs, out):
     nc = tc.nc
     with ExitStack() as ctx:
         keep = ctx.enter_context(tc.tile_pool(name="keep", bufs=1))
-        psum = ctx.enter_context(tc.psum_pool(name="psum", bufs=2))
+        psum = ctx.enter_context(tc.psum_pool(name="psum", bufs=3))
 
         offsets = keep.tile([P, J // 16], U16, name="offsets")
         nc.sync.dma_start(offsets[:], offs)
@@ -42,99 +43,124 @@ def tile_moe_expert_input_gradient_rectified_kernel(tc, g, sv, w_words, w_scales
         run_sb = [keep.tile([P, T], F32, name="run%d" % m) for m in range(K // P)]
         placed = [keep.tile([P, T], F32, name="placed%d" % m) for m in range(K // P)]
 
-        nc.vector.memset(scales[:].bitcast(I32), 0)
-        for m in range(K // P):
-            (nc.vector if m < 2 else nc.gpsimd).memset(placed[m][:], 0.0)
+        codes = keep.tile([P, HALF + PASSES * J], U32, name="codes", align_bytes=64)
+        d_scales = keep.tile([P, HALF + PASSES * J], U8, name="d_scales", align_bytes=64)
 
-        for i in range(PLANES + AHEAD):
-            if i < PLANES:
+        nc.vector.memset(scales[:].bitcast(I32), 0)
+        nc.gpsimd.memset(codes[:, :HALF], 0)
+        nc.gpsimd.memset(d_scales[:, :HALF].bitcast(I32), 0)
+        for m in range(K // P):
+            (nc.vector if m < 1 else nc.gpsimd).memset(placed[m][:], 0.0)
+
+        order = [("sv", 0), ("g", 0), ("sv", 1), ("g", 1), ("sv", 2), ("g", 2), ("sv", 3), ("g", 3),
+                 ("sv", 4), ("sv", 5), ("g", 4), ("sv", 6), ("sv", 7), ("g", 5), ("g", 6), ("g", 7)]
+        for kind, i in order:
+            if kind == "sv":
                 nc.sync.dma_start(sv_sb[i][:], sv_rows[i // PACK, i % PACK])
-            if i >= AHEAD:
-                nc.sync.dma_start(g_sb[i - AHEAD][:], g_rows[(i - AHEAD) // PACK, (i - AHEAD) % PACK])
+            else:
+                nc.sync.dma_start(g_sb[i][:], g_rows[i // PACK, i % PACK])
         nc.sync.dma_start(words[:].bitcast(I32), w_words.rearrange("z p b -> p z b").bitcast(I32))
         scale_rows = w_scales.rearrange("z (q r) c -> r q z c", r=4).bitcast(I32)
         for r in range(4):
             nc.sync.dma_start(scales[r:P:32].bitcast(I32), scale_rows[r])
-        for m in range(K // P):
+        for m in (1, 0, 2, 3):
             nc.sync.dma_start(run_sb[m][:], run[m * P:(m + 1) * P, :])
 
         picked = [keep.tile([P, J], F32, name="picked%d" % i) for i in range(PLANES)]
+        g_picked = [keep.tile([P, J], F32, name="g_picked%d" % i) for i in range(PLANES - FUSED)]
         rect = [keep.tile([P, J], F32, name="rect%d" % i) for i in range(PLANES)]
-        d32 = [keep.tile([P, PACK, J], F32, name="d32_%d" % z) for z in range(PASSES)]
-        d16 = [keep.tile([P, J, PACK], BF16, name="d16_%d" % z, align_bytes=64) for z in range(PASSES)]
-        codes = [keep.tile([P, J], U32, name="codes%d" % z, align_bytes=64) for z in range(PASSES)]
-        d_scales = [keep.tile([P, J], U8, name="d_scales%d" % z, align_bytes=64) for z in range(PASSES)]
+        d32_first = keep.tile([P, PACK, J], F32, name="d32_first")
+        d32_last = keep.tile([P, 2, PACK, HALF], F32, name="d32_last")
+        d16_first = keep.tile([P, J, PACK], BF16, name="d16_first", align_bytes=64)
+        d16_last = keep.tile([P, HALF, PACK], BF16, name="d16_last", align_bytes=64)
         prod = [keep.tile([P, J], F32, name="prod%d" % m) for m in range(K // P)]
+        last = PLANES - 1
+        rect_last_a = d32_last[:, 1].rearrange("p r j -> p (r j)")[:, HALF + QUARTER:2 * HALF + QUARTER]
+
+        def rect_half(i, h):
+            if i == last and h == 0:
+                return rect_last_a
+            return rect[i][:, h * HALF:(h + 1) * HALF]
 
         def pick_sv(i):
             nc.vector.tensor_copy(picked[i][:], sv_sb[i][:].indirect(offsets[:]))
-            nc.scalar.activation(rect[i][:], picked[i][:], ACT.Relu, scale=2.0)
+            if i == last:
+                for h in range(2):
+                    nc.scalar.activation(rect_half(i, h), picked[i][:, h * HALF:(h + 1) * HALF], ACT.Relu, scale=2.0)
+            else:
+                nc.scalar.activation(rect[i][:], picked[i][:], ACT.Relu, scale=2.0)
 
-        def product(i, lo, hi):
-            nc.vector.tensor_tensor(d32[i // PACK][:, i % PACK, lo:hi], g_sb[i][:].indirect(offsets[:, lo // 16:hi // 16]),
-                                    rect[i][:, lo:hi], ALU.mult)
+        def product_apart(i):
+            nc.vector.tensor_copy(g_picked[i][:], g_sb[i][:].indirect(offsets[:]))
+            if i < PACK:
+                nc.gpsimd.tensor_tensor(d32_first[:, i, :], g_picked[i][:], rect[i][:], ALU.mult)
+            else:
+                nc.gpsimd.tensor_tensor(d32_last[:, :, i - PACK, :], g_picked[i][:].rearrange("p (h j) -> p h j", h=2),
+                                        rect[i][:].rearrange("p (h j) -> p h j", h=2), ALU.mult)
 
-        def weave_scalar(z, lo, hi):
-            nc.scalar.copy(d16[z][:, lo:hi, :], d32[z][:, :, lo:hi].rearrange("p r j -> p j r"))
+        def product_fused(i, h):
+            nc.vector.tensor_tensor(d32_last[:, h, i - PACK, :],
+                                    g_sb[i][:].indirect(offsets[:, h * HALF // 16:(h + 1) * HALF // 16]),
+                                    rect_half(i, h), ALU.mult)
 
-        def weave_vector(z, lo, hi):
-            nc.vector.tensor_copy(d16[z][:, lo:hi, :], d32[z][:, :, lo:hi].rearrange("p r j -> p j r"))
+        def quantize(at, width, woven):
+            nc.vector.quantize_mx(out=codes[:, at:at + width].bitcast(E5M2), scales=d_scales[:, at:at + width],
+                                  in_=woven.rearrange("p j r -> p (j r)"))
 
-        def quantize(z, lo, hi):
-            nc.vector.quantize_mx(out=codes[z][:, lo:hi].bitcast(E5M2), scales=d_scales[z][:, lo:hi],
-                                  in_=d16[z][:, lo:hi, :].rearrange("p j r -> p (j r)"))
-
-        def multiply(acc, m, z):
+        def multiply(acc, m, z, at):
             nc.tensor.matmul_mx(out=acc[:], lhsT=words[:, z, 2 * P * m:2 * P * (m + 1)].bitcast(E2M1),
                                 lhsT_scale=scales[:, z, P * m:P * (m + 1)],
-                                rhs=codes[z][:].bitcast(E5M2), rhs_scale=d_scales[z][:],
+                                rhs=codes[:, at:at + J].bitcast(E5M2), rhs_scale=d_scales[:, at:at + J],
                                 start=(z == 0), stop=(z == PASSES - 1))
 
         def scatter(m, lo, hi):
             nc.vector.tensor_copy(placed[m][:].indirect(offsets[:, lo // 16:hi // 16]), prod[m][:, lo:hi])
 
-        def finish(engine, m, lo, hi):
+        def finish(engine, queue, m, lo, hi):
             engine.tensor_tensor(run_sb[m][:, lo:hi], placed[m][:, lo:hi], run_sb[m][:, lo:hi], ALU.add)
-            nc.sync.dma_start(out[m * P:(m + 1) * P, lo:hi], run_sb[m][:, lo:hi])
+            queue.dma_start(out[m * P:(m + 1) * P, lo:hi], run_sb[m][:, lo:hi])
 
-        for i in range(PLANES + AHEAD):
-            if i < PLANES:
+        for kind, i in order:
+            if kind == "sv":
                 pick_sv(i)
-            k = i - AHEAD
-            if 0 <= k < PLANES - 1:
-                product(k, 0, J)
-            if k == PACK - 1:
-                weave_scalar(0, 0, HALF)
-            if k == PACK:
-                weave_scalar(0, HALF, J)
-            if k == PACK + 1:
-                quantize(0, 0, J)
-        product(PLANES - 1, 0, HALF)
-        weave_scalar(1, 0, HALF)
-        product(PLANES - 1, HALF, J)
-        weave_vector(1, HALF, J)
-        quantize(1, 0, HALF)
-        quantize(1, HALF, J)
-
-        acc = []
-        for m in range(K // P):
-            acc.append(psum.tile([P, J], F32, name="acc"))
-            for z in range(PASSES):
-                multiply(acc[m], m, z)
-            if m == 0:
-                nc.scalar.copy(prod[0][:, :HALF], acc[0][:, :HALF])
+            elif i < PLANES - FUSED:
+                product_apart(i)
             else:
-                nc.scalar.copy(prod[m][:], acc[m][:])
-            if m == 1:
-                nc.scalar.copy(prod[0][:, HALF:], acc[0][:, HALF:])
+                product_fused(i, 0)
+            if kind == "g" and i == PACK - 1:
+                for h in range(2):
+                    nc.scalar.copy(d16_first[:, h * HALF:(h + 1) * HALF, :],
+                                   d32_first[:, :, h * HALF:(h + 1) * HALF].rearrange("p r j -> p j r"))
+                quantize(HALF, J, d16_first[:])
+        nc.scalar.copy(d16_last[:], d32_last[:, 0].rearrange("p r j -> p j r"))
+        for i in range(last, last - FUSED, -1):
+            product_fused(i, 1)
+        quantize(HALF + J, HALF, d16_last[:])
+
+        early = psum.tile([P, J], F32, name="acc")
+        for z in range(PASSES):
+            multiply(early, 0, z, z * J)
+
+        nc.scalar.copy(d16_last[:, :QUARTER, :], d32_last[:, 1, :, :QUARTER].rearrange("p r j -> p j r"))
+        nc.vector.tensor_copy(d16_last[:, QUARTER:, :], d32_last[:, 1, :, QUARTER:].rearrange("p r j -> p j r"))
+        quantize(HALF + J + HALF, HALF, d16_last[:])
+        nc.scalar.copy(prod[0][:, :HALF], early[:, HALF:])
+
+        for m in (1, 0, 2, 3):
+            acc = psum.tile([P, J], F32, name="acc")
+            for z in range(PASSES):
+                multiply(acc, m, z, HALF + z * J)
+            lo = HALF if m == 0 else 0
+            nc.scalar.copy(prod[m][:, lo:], acc[:, lo:])
 
         scatter(0, 0, HALF)
         scatter(1, 0, J)
-        finish(nc.gpsimd, 1, 0, T)
+        finish(nc.gpsimd, nc.sync, 1, 0, T)
         scatter(0, HALF, J)
-        finish(nc.gpsimd, 0, 0, T)
+        finish(nc.gpsimd, nc.sync, 0, 0, T)
         scatter(2, 0, J)
-        finish(nc.gpsimd, 2, 0, T)
+        finish(nc.gpsimd, nc.sync, 2, 0, T)
         scatter(3, 0, J)
-        finish(nc.vector, 3, 0, T // 2)
-        finish(nc.vector, 3, T // 2, T)
+        finish(nc.vector, nc.sync, 3, 0, T // 2)
+        finish(nc.vector, nc.scalar, 3, T // 2, 3 * T // 4)
+        finish(nc.vector, nc.sync, 3, 3 * T // 4, T)

from contextlib import ExitStack

import concourse.mybir as mybir

N, K, T, J = 1024, 512, 1024, 512
FLOPS = 2 * N * K * J

F32 = mybir.dt.float32
BF16 = mybir.dt.bfloat16
I32 = mybir.dt.int32
U32 = mybir.dt.uint32
U16 = mybir.dt.uint16
U8 = mybir.dt.uint8
E5M2 = mybir.dt.float8_e5m2_x4
E2M1 = mybir.dt.float4_e2m1fn_x4
ACT = mybir.ActivationFunctionType
ALU = mybir.AluOpType

P = 128
PACK = 4
PASSES = N // (P * PACK)
PLANES = PASSES * PACK
HALF = J // 2
QUARTER = J // 4
FUSED = 3


def tile_moe_expert_input_gradient_rectified_kernel(tc, g, sv, w_words, w_scales, run, offs, out):
    nc = tc.nc
    with ExitStack() as ctx:
        keep = ctx.enter_context(tc.tile_pool(name="keep", bufs=1))
        psum = ctx.enter_context(tc.psum_pool(name="psum", bufs=3))

        offsets = keep.tile([P, J // 16], U16, name="offsets")
        nc.sync.dma_start(offsets[:], offs)

        g_rows = g.rearrange("(z p r) t -> z r p t", z=PASSES, r=PACK)
        sv_rows = sv.rearrange("(z p r) t -> z r p t", z=PASSES, r=PACK)
        g_sb = [keep.tile([P, T], F32, name="g%d" % i) for i in range(PLANES)]
        sv_sb = [keep.tile([P, T], F32, name="sv%d" % i) for i in range(PLANES)]
        words = keep.tile([P, PASSES, 2 * K], U8, name="words", align_bytes=64)
        scales = keep.tile([P, PASSES, K], U8, name="scales", align_bytes=64)
        run_sb = [keep.tile([P, T], F32, name="run%d" % m) for m in range(K // P)]
        placed = [keep.tile([P, T], F32, name="placed%d" % m) for m in range(K // P)]

        codes = keep.tile([P, HALF + PASSES * J], U32, name="codes", align_bytes=64)
        d_scales = keep.tile([P, HALF + PASSES * J], U8, name="d_scales", align_bytes=64)

        nc.vector.memset(scales[:].bitcast(I32), 0)
        nc.gpsimd.memset(codes[:, :HALF], 0)
        nc.gpsimd.memset(d_scales[:, :HALF].bitcast(I32), 0)
        for m in range(K // P):
            (nc.vector if m < 1 else nc.gpsimd).memset(placed[m][:], 0.0)

        order = [("sv", 0), ("g", 0), ("sv", 1), ("g", 1), ("sv", 2), ("g", 2), ("sv", 3), ("g", 3),
                 ("sv", 4), ("sv", 5), ("g", 4), ("sv", 6), ("sv", 7), ("g", 5), ("g", 6), ("g", 7)]
        for kind, i in order:
            if kind == "sv":
                nc.sync.dma_start(sv_sb[i][:], sv_rows[i // PACK, i % PACK])
            else:
                nc.sync.dma_start(g_sb[i][:], g_rows[i // PACK, i % PACK])
        nc.sync.dma_start(words[:].bitcast(I32), w_words.rearrange("z p b -> p z b").bitcast(I32))
        scale_rows = w_scales.rearrange("z (q r) c -> r q z c", r=4).bitcast(I32)
        for r in range(4):
            nc.sync.dma_start(scales[r:P:32].bitcast(I32), scale_rows[r])
        for m in (1, 0, 2, 3):
            nc.sync.dma_start(run_sb[m][:], run[m * P:(m + 1) * P, :])

        picked = [keep.tile([P, J], F32, name="picked%d" % i) for i in range(PLANES)]
        g_picked = [keep.tile([P, J], F32, name="g_picked%d" % i) for i in range(PLANES - FUSED)]
        rect = [keep.tile([P, J], F32, name="rect%d" % i) for i in range(PLANES)]
        d32_first = keep.tile([P, PACK, J], F32, name="d32_first")
        d32_last = keep.tile([P, 2, PACK, HALF], F32, name="d32_last")
        d16_first = keep.tile([P, J, PACK], BF16, name="d16_first", align_bytes=64)
        d16_last = keep.tile([P, HALF, PACK], BF16, name="d16_last", align_bytes=64)
        prod = [keep.tile([P, J], F32, name="prod%d" % m) for m in range(K // P)]
        last = PLANES - 1
        rect_last_a = d32_last[:, 1].rearrange("p r j -> p (r j)")[:, HALF + QUARTER:2 * HALF + QUARTER]

        def rect_half(i, h):
            if i == last and h == 0:
                return rect_last_a
            return rect[i][:, h * HALF:(h + 1) * HALF]

        def pick_sv(i):
            nc.vector.tensor_copy(picked[i][:], sv_sb[i][:].indirect(offsets[:]))
            if i == last:
                for h in range(2):
                    nc.scalar.activation(rect_half(i, h), picked[i][:, h * HALF:(h + 1) * HALF], ACT.Relu, scale=2.0)
            else:
                nc.scalar.activation(rect[i][:], picked[i][:], ACT.Relu, scale=2.0)

        def product_apart(i):
            nc.vector.tensor_copy(g_picked[i][:], g_sb[i][:].indirect(offsets[:]))
            if i < PACK:
                nc.gpsimd.tensor_tensor(d32_first[:, i, :], g_picked[i][:], rect[i][:], ALU.mult)
            else:
                nc.gpsimd.tensor_tensor(d32_last[:, :, i - PACK, :], g_picked[i][:].rearrange("p (h j) -> p h j", h=2),
                                        rect[i][:].rearrange("p (h j) -> p h j", h=2), ALU.mult)

        def product_fused(i, h):
            nc.vector.tensor_tensor(d32_last[:, h, i - PACK, :],
                                    g_sb[i][:].indirect(offsets[:, h * HALF // 16:(h + 1) * HALF // 16]),
                                    rect_half(i, h), ALU.mult)

        def quantize(at, width, woven):
            nc.vector.quantize_mx(out=codes[:, at:at + width].bitcast(E5M2), scales=d_scales[:, at:at + width],
                                  in_=woven.rearrange("p j r -> p (j r)"))

        def multiply(acc, m, z, at):
            nc.tensor.matmul_mx(out=acc[:], lhsT=words[:, z, 2 * P * m:2 * P * (m + 1)].bitcast(E2M1),
                                lhsT_scale=scales[:, z, P * m:P * (m + 1)],
                                rhs=codes[:, at:at + J].bitcast(E5M2), rhs_scale=d_scales[:, at:at + J],
                                start=(z == 0), stop=(z == PASSES - 1))

        def scatter(m, lo, hi):
            nc.vector.tensor_copy(placed[m][:].indirect(offsets[:, lo // 16:hi // 16]), prod[m][:, lo:hi])

        def finish(engine, queue, m, lo, hi):
            engine.tensor_tensor(run_sb[m][:, lo:hi], placed[m][:, lo:hi], run_sb[m][:, lo:hi], ALU.add)
            queue.dma_start(out[m * P:(m + 1) * P, lo:hi], run_sb[m][:, lo:hi])

        for kind, i in order:
            if kind == "sv":
                pick_sv(i)
            elif i < PLANES - FUSED:
                product_apart(i)
            else:
                product_fused(i, 0)
            if kind == "g" and i == PACK - 1:
                for h in range(2):
                    nc.scalar.copy(d16_first[:, h * HALF:(h + 1) * HALF, :],
                                   d32_first[:, :, h * HALF:(h + 1) * HALF].rearrange("p r j -> p j r"))
                quantize(HALF, J, d16_first[:])
        nc.scalar.copy(d16_last[:], d32_last[:, 0].rearrange("p r j -> p j r"))
        for i in range(last, last - FUSED, -1):
            product_fused(i, 1)
        quantize(HALF + J, HALF, d16_last[:])

        early = psum.tile([P, J], F32, name="acc")
        for z in range(PASSES):
            multiply(early, 0, z, z * J)

        nc.scalar.copy(d16_last[:, :QUARTER, :], d32_last[:, 1, :, :QUARTER].rearrange("p r j -> p j r"))
        nc.vector.tensor_copy(d16_last[:, QUARTER:, :], d32_last[:, 1, :, QUARTER:].rearrange("p r j -> p j r"))
        quantize(HALF + J + HALF, HALF, d16_last[:])
        nc.scalar.copy(prod[0][:, :HALF], early[:, HALF:])

        for m in (1, 0, 2, 3):
            acc = psum.tile([P, J], F32, name="acc")
            for z in range(PASSES):
                multiply(acc, m, z, HALF + z * J)
            lo = HALF if m == 0 else 0
            nc.scalar.copy(prod[m][:, lo:], acc[:, lo:])

        scatter(0, 0, HALF)
        scatter(1, 0, J)
        finish(nc.gpsimd, nc.sync, 1, 0, T)
        scatter(0, HALF, J)
        finish(nc.gpsimd, nc.sync, 0, 0, T)
        scatter(2, 0, J)
        finish(nc.gpsimd, nc.sync, 2, 0, T)
        scatter(3, 0, J)
        finish(nc.vector, nc.sync, 3, 0, T // 2)
        finish(nc.vector, nc.scalar, 3, T // 2, 3 * T // 4)
        finish(nc.vector, nc.sync, 3, 3 * T // 4, T)
